import numpy as np, ml_dtypes
CORES = [12,28,60,100,156,228]
N = 6
import mx_ref
BF = ml_dtypes.bfloat16
def entries(a):
    return np.ascontiguousarray(a.T).reshape(-1)
def table(e):
    return np.ascontiguousarray(np.reshape(e, (-1, 16)).T).astype(np.int32)
def cols(t, e):
    v = np.concatenate([t.reshape(128, -1, 4), np.zeros((128, 1, 4), BF)], axis=1)
    return np.ascontiguousarray(v[:, e]).reshape(128, -1)
def f(rng, *shape):
    return mx_ref.flush((rng.standard_normal(shape, dtype=np.float32) * np.exp2(rng.integers(-2, 3, shape[:-1] + (1,)))).astype(BF))
def wide(rng, *shape, cols=0):
    v = rng.standard_normal(shape, dtype=np.float32) * np.exp2(rng.integers(-12, 13, shape)).astype(np.float32)
    if cols: v *= np.repeat(np.exp2(rng.integers(-cols, cols + 1, shape[:-2] + (1, shape[-1] // 4))) * (rng.random(shape[:-2] + (1, shape[-1] // 4)) > 0.0625), 4, axis=-1).astype(np.float32)
    return mx_ref.flush(v.astype(BF))
T, CAPP = 256, 64
def even(n):
    return [T // n + (k < T % n) for k in range(n)]
def counts(rng, h, moves=10 * N * N):
    n = np.array([[h[(d - s) % N] for d in range(N)] for s in range(N)])[rng.permutation(N)][:, rng.permutation(N)]
    top = np.where(n > 0, CAPP, 0)
    for _ in range(moves):
        a, b = rng.permutation(N)[:2]; c, e = rng.permutation(N)[:2]
        k = rng.integers(0, min(n[a, e], n[b, c], top[a, c] - n[a, c], top[b, e] - n[b, e]) + 1)
        n[a, c] += k; n[b, e] += k; n[a, e] -= k; n[b, c] -= k
    return n
def lists(rng, n, back=False):
    a = np.full((N, N, CAPP), -1)
    for s in range(N):
        p = np.arange(T)[::-1] if back else rng.permutation(T)
        for d in range(N):
            k = rng.permutation(CAPP)[:n[s, d]]
            if back: k = np.sort(k)
            a[s, d, k] = p[:n[s, d]]; p = p[n[s, d]:]
    m = []
    for d in range(N):
        k = np.flatnonzero(a[:, d].reshape(-1) >= 0)
        m.append(table(k[::-1] if back else rng.permutation(k)))
    return {"send": np.stack([table(a[s].reshape(-1)) for s in range(N)]), "mine": np.stack(m), "prev": np.stack([m[(r - 1) % N] for r in range(N)])}
def setup_inputs(rng):
    return {"x": f(rng, N, 128, 4 * T), **lists(rng, counts(rng, even(N)))}
def setup_inputs_empty(rng):
    return {**setup_inputs(rng), **lists(rng, counts(rng, even(N - 1) + [0]))}
def setup_inputs_full(rng):
    return {**setup_inputs(rng), **lists(rng, counts(rng, [min(CAPP, max(0, T - k * CAPP)) for k in range(N)], 0))}
def setup_inputs_reversed(rng):
    return {**setup_inputs(rng), **lists(rng, counts(rng, even(N)), back=True)}
def setup_inputs_spread(rng):
    d = setup_inputs(rng); d["x"] = wide(rng, N, 128, 4 * T, cols=8); return d
def check_inputs(d):
    b = []
    v = np.abs(np.asarray(d["x"]).astype(np.float32))
    if not ((v == 0) | ((v >= 2.0 ** -30) & (v <= 2.0 ** 30))).all(): b.append("x")
    for r in range(N):
        c, m = entries(d["send"][r]), entries(d["mine"][r])
        if c.min() < -1 or not np.array_equal(np.sort(c[c >= 0]), np.arange(T)): b.append("send")
        arrived = np.concatenate([entries(d["send"][s])[r * CAPP:(r + 1) * CAPP] for s in range(N)])
        if not np.array_equal(np.sort(m), np.flatnonzero(arrived >= 0)): b.append("mine")
        if not np.array_equal(d["prev"][r], d["mine"][(r - 1) % N]): b.append("prev")
    return b
def reference(x, send, mine, prev):
    K = []
    for r in range(N):
        arrived = np.concatenate([cols(x[s], entries(send[s])[r * CAPP:(r + 1) * CAPP]) for s in range(N)], axis=1)
        K.append(cols(arrived, entries(mine[r])))
    Q = [mx_ref.quantize(t) for t in K]
    y = np.zeros((N, T, 2 * T), np.float32)
    for r in range(N):
        for p in range(T // 128):
            W = mx_ref.quantize(np.ascontiguousarray(K[r][:, 512 * p:512 * p + 512]))
            y[r, 128 * p:128 * p + 128, :T] = mx_ref.matmul(W, Q[r])
            y[r, 128 * p:128 * p + 128, T:] = mx_ref.matmul(W, Q[(r - 1) % N])
    return {"y": y}

@@ -1,0 +1,325 @@
+from concourse.bass import DstId, RemoteDMATransfer, IndirectOffsetOnAxis
+from concourse.mybir import dt, AluOpType, AxisListType, ActivationFunctionType
+
+N, TC, CAP = 6, 256, 64
+W = 7 * CAP
+FAR = 512.0
+
+SCRATCH = {
+    "xs": ("sbuf", [128, 4 * TC], "bfloat16"),
+    "raw": ("sbuf", [64, N, 4], "int32"),
+    "off": ("sbuf", [128, 24], "uint16"),
+    "h": ("sbuf", [128, 4 * W], "bfloat16"),
+    "qc": ("sbuf", [128, W], "float8_e4m3fn_x4"),
+    "qs": ("sbuf", [128, W], "uint8"),
+    "lc": ("sbuf", [128, 768], "float8_e4m3fn_x4"),
+    "ls": ("sbuf", [128, 768], "uint8"),
+    "hc": ("sbuf", [128, 128], "float8_e4m3fn_x4"),
+    "hp": ("sbuf", [128, 128], "uint8"),
+    "ml": ("sbuf", [64, 32], "int32"),
+    "tm": ("sbuf", [64, 32 * 6], "int32"),
+    "oo": ("sbuf", [128, 32], "uint16"),
+    "jv": ("sbuf", [128, TC], "bfloat16"),
+    "inv": ("sbuf", [128, 768], "bfloat16"),
+    "o3i": ("sbuf", [128, 3], "int32"),
+    "o3": ("sbuf", [128, 4], "uint16"),
+    "mki": ("sbuf", [128, 48], "int32"),
+    "mkb": ("sbuf", [128, 48], "int32"),
+    "mk": ("sbuf", [128, 48], "float32"),
+    "ge": ("sbuf", [128, 48], "float32"),
+    "gm": ("sbuf", [128, 48], "float32"),
+    "rf": ("sbuf", [128, 4], "float32"),
+    "idx": ("sbuf", [128, 4], "int32"),
+}
+for _k in range(3):
+    SCRATCH["s%d" % _k] = ("sbuf", [128, 768], "float32")
+    SCRATCH["yt%d" % _k] = ("sbuf", [128, 2 * TC], "float32")
+for _k in range(7):
+    SCRATCH["ps%d" % _k] = ("psum", [128, 512], "float32")
+
+SEMAPHORES = ["lsend", "lx", "llist", "offr", "sg", "q1", "q2", "ql", "gi", "offo", "idxr", "v",
+              "arr0", "arr1", "arr2", "loc", "st", "hcs", "hss", "hl",
+              "sv0", "sv1", "sv2", "ss0", "ss1", "ss2", "yr0", "yr1", "yr2"] + ["m%d" % k for k in range(7)]
+
+
+def bits(es):
+    m = 0
+    for e in es:
+        m |= 1 << e
+    return m
+
+
+def make_plan(cores, topo):
+    direct = [[t for t in range(N) if t != s and topo.may_write(cores[s], cores[t])] for s in range(N)]
+    most = max(len(d) for d in direct)
+    major = [s for s in range(N) if len(direct[s]) == most]
+    minor = [s for s in range(N) if len(direct[s]) != most]
+    slots = [(major[1], major[0]), (major[3], major[2]), (minor[0], minor[1])]
+    rising = [a for a, b in slots]
+    place = {}
+    for k in range(3):
+        for j in range(2):
+            place[slots[k][j]] = (k, 256 * k + 128 * j)
+    road = {}
+    for s in range(N):
+        me = cores[s]
+        relay = [t for t in range(N) if t != s and t not in direct[s]]
+        flip = (major if s in major else minor).index(s) % 2
+        sets = [[c for c in topo.cores_of(me) if c != me and topo.may_write(c, cores[relay[0]])
+                 and (topo.die(c) != topo.die(me)) == bool(other)] for other in (0, 1)]
+        half = (len(relay) + 1) // 2
+        used = [0, 0]
+        on = topo.engines(me, sets[0][0])
+        far = topo.engines(me, cores[direct[s][0]])
+        free = [e for e in on if e not in far] if len(relay) <= 2 else on
+        per = len(free) // len(relay)
+        for i, t in enumerate(relay):
+            d = (0 if i < half else 1) ^ flip
+            c = sets[d][used[d]]
+            used[d] += 1
+            road[s, t] = {"helper": c, "hop": free[per * i:per * i + per], "codes": topo.engines(c, cores[t]),
+                          "scales": topo.engines(c, cores[t])}
+        n = len(far)
+        if len(direct[s]) == 1:
+            road[s, direct[s][0]] = {"helper": None, "codes": far, "scales": far}
+        else:
+            h, q = n // 2, n // 4
+            cs = [far[:h], far[h:h + q], far[h + q:]]
+            ss = [far[h:], far[:q], far[q:h]]
+            for i in range(3):
+                t = major[(major.index(s) + 1 + i) % len(major)]
+                road[s, t] = {"helper": None, "codes": cs[i], "scales": ss[i]}
+    return direct, major, slots, rising, place, road
+
+
+def rank_program(g, core, T, topo):
+    cores = list(T.cores)
+    plan = make_plan(cores, topo)
+    rank = T.rank_of(core)
+    if rank is not None:
+        sender(g, core, T, topo, cores, rank, plan)
+        return
+    place, road = plan[4], plan[5]
+    for (s, t), r in road.items():
+        if r["helper"] == core:
+            helper(g, core, T, topo, cores, r, t, place[s])
+
+
+def helper(g, core, T, topo, cores, r, t, at):
+    slot, base = at
+    rid, pid = topo.addr(cores[t], core)
+    arr = T.sem["arr%d" % slot]
+    n = len(r["hop"])
+    g.wait_ge(T.sem.hss, n)
+    g.remote_dma(T.ls[:, base:base + 128], T.hp[:, 0:128], arr, T.sem.hl, pid, rid, bits(r["scales"]))
+    g.wait_ge(T.sem.hcs, n)
+    g.remote_dma(T.lc[:, base:base + 128].bitcast(dt.uint8), T.hc[:, 0:128].bitcast(dt.uint8), arr, T.sem.hl, pid, rid,
+                 bits(r["codes"]))
+    g.wait_ge(T.sem.hl, len(r["scales"]) + len(r["codes"]))
+
+
+def sender(g, core, T, topo, cores, s, plan):
+    direct, major, slots, rising, place, road = plan
+    sem = T.sem
+    V, S, X = g.vector, g.scalar, g.sync
+    A = AluOpType
+    copy = ActivationFunctionType.Copy
+    up = s in rising
+    cnt = {"v": 0}
+
+    def tick(ins):
+        ins.then_inc(sem.v, 1)
+        cnt["v"] += 1
+
+    def tock():
+        V.wait_ge(sem.v, cnt["v"])
+
+    def col(t):
+        return CAP * t if up else CAP * (N - 1 - t)
+
+    X.dma_start(T.xs[:, :], T.x[:, :]).then_inc(sem.lx, 16)
+    for q in range(4):
+        (S, X)[q % 2].dma_start(T.raw[16 * q:16 * q + 16, :, :], T.send[:, :]).then_inc(sem.lsend, 16)
+    for q in range(4):
+        X.dma_start(T.ml[16 * q:16 * q + 16, 0:16], T.mine[:, :]).then_inc(sem.llist, 16)
+        X.dma_start(T.ml[16 * q:16 * q + 16, 16:32], T.prev[:, :]).then_inc(sem.llist, 16)
+
+    g.iota(T.o3i[:, 0:3], [[256, 3]], CAP, 1).then_inc(sem.gi, 1)
+    g.iota(T.mki[:, 0:48], [[0, 3], [1, 16]], 128, -1).then_inc(sem.gi, 1)
+    g.iota(T.jv[:, 0:TC], [[1, TC]], 0, 0, allow_small_or_imprecise_dtypes=True).then_inc(sem.gi, 1)
+    tick(V.memset(T.inv[:, 0:768], FAR))
+    V.wait_ge(sem.gi, 3)
+    tick(V.tensor_copy(T.o3[:, 0:3], T.o3i[:, 0:3]))
+    tick(V.tensor_scalar(T.mkb[:, 0:48], T.mki[:, 0:48], 15, None, A.bitwise_and))
+    tock()
+    tick(V.tensor_scalar(T.mk[:, 0:48], T.mkb[:, 0:48], 0.0, None, A.is_equal))
+
+    V.wait_ge(sem.lsend, 64)
+    src = T.raw[:, :, :] if up else T.raw[:, ::-1, :]
+    for p in (0, 64):
+        V.tensor_scalar(T.off[p:p + 64, 0:24], src, 4.0, 0.0, A.mult, A.max).then_inc(sem.offr, 1)
+
+    first = 4 * CAP if up else 0
+    last = first + 4 * CAP * N
+    for q in (V, S):
+        q.wait_ge(sem.lx, 16)
+        q.wait_ge(sem.offr, 2)
+    for t in range(4):
+        win = T.xs[:, t:4 * TC].indirect(T.off[:, 0:24])
+        if t < 2:
+            tick(V.tensor_copy(T.h[:, first + t:last:4], win))
+        else:
+            S.activation(T.h[:, first + t:last:4], win, copy).then_inc(sem.sg, 1)
+    V.wait_ge(sem.sg, 2)
+    tock()
+
+    relay = [t for t in range(N) if t != s and t not in direct[s]]
+
+    def double():
+        z, e = T.h[:, 0:4 * CAP], T.h[:, 4 * CAP * N:4 * W]
+        tick(V.tensor_copy(z, e) if up else V.tensor_copy(e, z))
+        tock()
+
+    def pack(a, b, which):
+        V.quantize_mx(T.qc[:, a:b], T.qs[:, a:b], T.h[:, 4 * a:4 * b]).then_inc(which, 1)
+
+    n2 = 0
+    if len(relay) == 2:
+        a = min(col(t) for t in relay)
+        b = max(col(t) for t in relay) + 128
+        pack(a, b, sem.q1)
+        double()
+        for lo, hi in ((0, a), (b, W)):
+            if hi > lo:
+                pack(lo, hi, sem.q2)
+                n2 += 1
+    else:
+        double()
+        pack(0, W, sem.q1)
+    slot, at = place[s]
+    V.quantize_mx(T.lc[:, at:at + 128], T.ls[:, at:at + 128], T.h[:, 4 * col(s):4 * col(s) + 512]).then_inc(sem.ql, 1)
+
+    local = 0
+    for step in range(4):
+        far, codes = step > 1, step in (1, 2)
+        if step == 0:
+            g.wait_ge(sem.q1, 1)
+        if step == 2 and n2:
+            g.wait_ge(sem.q2, n2)
+        trs = []
+        for t in (direct[s] if far else relay):
+            r, c0 = road[s, t], col(t)
+            es = r["hop"] if not far else r["codes"] if codes else r["scales"]
+            to = cores[t] if far else r["helper"]
+            rid, pid = topo.addr(to, core)
+            if codes:
+                a_ = T.qc[:, c0:c0 + 128].bitcast(dt.uint8)
+                b_ = (T.lc[:, at:at + 128] if far else T.hc[:, 0:128]).bitcast(dt.uint8)
+            else:
+                a_ = T.qs[:, c0:c0 + 128]
+                b_ = T.ls[:, at:at + 128] if far else T.hp[:, 0:128]
+            m_ = sem["arr%d" % slot] if far else sem.hcs if codes else sem.hss
+            trs.append(RemoteDMATransfer(dst_ids=[DstId(rid=rid, pnc=pid)], dma_engine_mask=bits(es), remote_sem=m_,
+                                         src=a_, dst=b_))
+            local += len(es)
+        g.remote_dma_fused(trs, local_sem=sem.loc)
+
+    own, pre = [], []
+    for r in range(N):
+        b = place[r][1] - CAP * r
+        own.append(b + (CAP if r in rising else 0))
+        pre.append(b + (0 if r in rising else CAP))
+    V.wait_ge(sem.llist, 128)
+    for i in range(N):
+        for half, tab in ((0, own), (16, pre)):
+            o_, i_ = T.tm[:, 32 * i + half:32 * i + half + 16], T.ml[:, half:half + 16]
+            if i == 0:
+                tick(V.tensor_scalar(o_, i_, float(tab[0]), None, A.add))
+            else:
+                tick(V.tensor_scalar(o_, i_, float(CAP * i), float(tab[i] - tab[i - 1]), A.is_ge, A.mult))
+    tock()
+    for lo, n in ((96, 96), (32, 32), (64, 32)):
+        tick(V.tensor_tensor(T.tm[:, 0:n], T.tm[:, 0:n], T.tm[:, lo:lo + n], A.add))
+        tock()
+    for p in (0, 64):
+        V.tensor_copy(T.oo[p:p + 64, 0:32], T.tm[:, 0:32]).then_inc(sem.offo, 1)
+    V.wait_ge(sem.offo, 2)
+    om, op = T.oo[:, 0:16], T.oo[:, 16:32]
+
+    tick(V.tensor_copy(T.inv[:, 0:768].indirect(om), T.jv[:, 0:TC]))
+    tock()
+    tick(V.tensor_copy(T.ge[:, 0:48], T.inv[:, 0:768].indirect(T.o3[:, 0:3])))
+    tock()
+    tick(V.tensor_tensor(T.gm[:, 0:48], T.ge[:, 0:48], T.mk[:, 0:48], A.mult))
+    tock()
+    for k in range(3):
+        tick(V.tensor_reduce(T.rf[:, k:k + 1], T.gm[:, 16 * k:16 * k + 16], AxisListType.X, A.add))
+    tock()
+    V.tensor_copy(T.idx[:, 0:3], T.rf[:, 0:3]).then_inc(sem.idxr, 1)
+
+    wait_for = [sum(len(road[a, s]["codes"]) + len(road[a, s]["scales"]) for a in slots[k] if a != s) for k in range(3)]
+    if s in major:
+        early, order = [0, 1], [0, 1, 2]
+        pieces = {0: [(0, 512, "V"), (512, 768, "V")], 1: [(0, 512, "S"), (512, 768, "S")],
+                  2: [(0, 512, "V"), (512, 768, "S")]}
+        soon = [(0, 0), (1, 0)]
+        vq = [(0, 0), (0, 1), (0,), (2, 0), (1,), (2,)]
+        sq = [(1, 0), (0,), (1, 1), (1,), (2, 1), (2,)]
+    else:
+        early, order = [2], [2, 0, 1]
+        pieces = {2: [(512, 768, "S"), (0, 256, "V"), (256, 512, "S")], 0: [(0, 512, "V"), (512, 768, "S")],
+                  1: [(0, 512, "V"), (512, 768, "S")]}
+        soon = [(2, 0)]
+        vq = [(2, 1), (2,), (0, 0), (0,), (1, 0), (1,)]
+        sq = [(2, 0), (2, 2), (2,), (0, 1), (0,), (1, 1), (1,)]
+    todo = soon + [(k, i) for k in order for i in range(len(pieces[k])) if (k, i) not in soon]
+    bank = {}
+    g.tensor.wait_ge(sem.ql, 1)
+    for k in early:
+        g.tensor.wait_ge(sem["arr%d" % k], wait_for[k])
+    for k, i in todo:
+        if len(bank) == len(soon):
+            for e in range(3):
+                if e not in early:
+                    g.tensor.wait_ge(sem["arr%d" % e], wait_for[e])
+        b = bank[k, i] = len(bank)
+        a, z, who = pieces[k][i]
+        w0 = 256 * k + CAP
+        g.tensor.matmul_mx(T["ps%d" % b][:, 0:z - a], T.lc[:, w0:w0 + 128], T.ls[:, w0:w0 + 128], T.lc[:, a:z], T.ls[:, a:z],
+                           True, True).then_inc(sem["m%d" % b], 1)
+
+    def after(q, steps):
+        for st in steps:
+            k = st[0]
+            sk, yk = T["s%d" % k], T["yt%d" % k]
+            if len(st) == 2:
+                a, z, w = pieces[k][st[1]]
+                b = bank[k, st[1]]
+                q.wait_ge(sem["m%d" % b], 1)
+                if q is V:
+                    q.tensor_copy(sk[:, a:z], T["ps%d" % b][:, 0:z - a]).then_inc(sem["sv%d" % k], 1)
+                else:
+                    q.activation(sk[:, a:z], T["ps%d" % b][:, 0:z - a], copy).then_inc(sem["ss%d" % k], 1)
+                continue
+            for w, name in (("V", "sv%d"), ("S", "ss%d")):
+                n = len([p for p in pieces[k] if p[2] == w])
+                if n:
+                    q.wait_ge(sem[name % k], n)
+            if q is V:
+                q.tensor_copy(yk[:, 0:TC], sk[:, 0:768].indirect(om)).then_inc(sem["yr%d" % k], 1)
+            else:
+                q.activation(yk[:, TC:2 * TC], sk[:, 0:768].indirect(op), copy).then_inc(sem["yr%d" % k], 1)
+
+    S.wait_ge(sem.offo, 2)
+    after(V, vq)
+    after(S, sq)
+    V.wait_ge(sem.v, cnt["v"])
+
+    g.wait_ge(sem.idxr, 1)
+    for k in order:
+        g.wait_ge(sem["yr%d" % k], 2)
+        g.indirect_dma_start(out=T.y[:], out_offset=IndirectOffsetOnAxis(ap=T.idx[:, k:k + 1], axis=0),
+                             in_=T["yt%d" % k][:, 0:2 * TC], in_offset=None, bounds_check=TC - 1,
+                             oob_is_err=False).then_inc(sem.st, 16)
+    g.wait_ge(sem.st, 48)
+    g.wait_ge(sem.loc, local)

@@ -1,17 +1,16 @@
 from concourse.bass import DstId, RemoteDMATransfer, IndirectOffsetOnAxis
-from concourse.mybir import dt, AluOpType, AxisListType, ActivationFunctionType
+from concourse.mybir import dt, AluOpType, ActivationFunctionType
 
 N, TC, CAP = 6, 256, 64
-W = 7 * CAP
-FAR = 512.0
+FAR = 512
 
 SCRATCH = {
     "xs": ("sbuf", [128, 4 * TC], "bfloat16"),
     "raw": ("sbuf", [64, N, 4], "int32"),
     "off": ("sbuf", [128, 24], "uint16"),
-    "h": ("sbuf", [128, 4 * W], "bfloat16"),
-    "qc": ("sbuf", [128, W], "float8_e4m3fn_x4"),
-    "qs": ("sbuf", [128, W], "uint8"),
+    "h": ("sbuf", [128, 4 * CAP * (N + 1)], "bfloat16"),
+    "qc": ("sbuf", [128, CAP * N], "float8_e4m3fn_x4"),
+    "qs": ("sbuf", [128, CAP * N], "uint8"),
     "lc": ("sbuf", [128, 768], "float8_e4m3fn_x4"),
     "ls": ("sbuf", [128, 768], "uint8"),
     "hc": ("sbuf", [128, 128], "float8_e4m3fn_x4"),
@@ -19,16 +18,8 @@ SCRATCH = {
     "ml": ("sbuf", [64, 32], "int32"),
     "tm": ("sbuf", [64, 32 * 6], "int32"),
     "oo": ("sbuf", [128, 32], "uint16"),
-    "jv": ("sbuf", [128, TC], "bfloat16"),
-    "inv": ("sbuf", [128, 768], "bfloat16"),
-    "o3i": ("sbuf", [128, 3], "int32"),
-    "o3": ("sbuf", [128, 4], "uint16"),
-    "mki": ("sbuf", [128, 48], "int32"),
-    "mkb": ("sbuf", [128, 48], "int32"),
-    "mk": ("sbuf", [128, 48], "float32"),
-    "ge": ("sbuf", [128, 48], "float32"),
-    "gm": ("sbuf", [128, 48], "float32"),
-    "rf": ("sbuf", [128, 4], "float32"),
+    "jv": ("sbuf", [128, TC], "int32"),
+    "inv": ("sbuf", [128, 768], "int32"),
     "idx": ("sbuf", [128, 4], "int32"),
 }
 for _k in range(3):
@@ -37,7 +28,7 @@ for _k in range(3):
 for _k in range(7):
     SCRATCH["ps%d" % _k] = ("psum", [128, 512], "float32")
 
-SEMAPHORES = ["lsend", "lx", "llist", "offr", "sg", "q1", "q2", "ql", "gi", "offo", "idxr", "v",
+SEMAPHORES = ["lsend", "lx", "llist", "offr", "sg0", "sg1", "q1", "q2", "ql", "gi", "offo", "iv", "idxr", "v",
               "arr0", "arr1", "arr2", "loc", "st", "hcs", "hss", "hl",
               "sv0", "sv1", "sv2", "ss0", "ss1", "ss2", "yr0", "yr1", "yr2"] + ["m%d" % k for k in range(7)]
 
@@ -54,9 +45,9 @@ def make_plan(cores, topo):
     most = max(len(d) for d in direct)
     major = [s for s in range(N) if len(direct[s]) == most]
     minor = [s for s in range(N) if len(direct[s]) != most]
-    slots = [(major[1], major[0]), (major[3], major[2]), (minor[0], minor[1])]
+    slots = [(major[0], major[1]), (major[2], major[3]), (minor[0], minor[1])]
     rising = [a for a, b in slots]
-    place = {}
+    place, pos, chunks, lead = {}, {}, {}, {}
     for k in range(3):
         for j in range(2):
             place[slots[k][j]] = (k, 256 * k + 128 * j)
@@ -64,6 +55,11 @@ def make_plan(cores, topo):
     for s in range(N):
         me = cores[s]
         relay = [t for t in range(N) if t != s and t not in direct[s]]
+        for t in range(N):
+            pos[s, t] = (t - 1 - s) % N if s in rising else (s - 1 - t) % N
+        size, t0, front = min([(pos[s, t] + 2, t, True) for t in relay] + [(N - pos[s, t], t, False) for t in relay])
+        lead[s] = t0
+        chunks[s] = [(0, size), (size, N)] if front else [(N - size, N), (0, N - size)]
         flip = (major if s in major else minor).index(s) % 2
         sets = [[c for c in topo.cores_of(me) if c != me and topo.may_write(c, cores[relay[0]])
                  and (topo.die(c) != topo.die(me)) == bool(other)] for other in (0, 1)]
@@ -71,17 +67,19 @@ def make_plan(cores, topo):
         used = [0, 0]
         on = topo.engines(me, sets[0][0])
         far = topo.engines(me, cores[direct[s][0]])
-        free = [e for e in on if e not in far] if len(relay) <= 2 else on
+        free = [e for e in on if e not in far] if len(relay) <= 2 else far + [e for e in on if e not in far]
         per = len(free) // len(relay)
+        turn = [t0] + [t for t in relay if t != t0]
         for i, t in enumerate(relay):
             d = (0 if i < half else 1) ^ flip
             c = sets[d][used[d]]
             used[d] += 1
-            road[s, t] = {"helper": c, "hop": free[per * i:per * i + per], "codes": topo.engines(c, cores[t]),
+            j = turn.index(t)
+            road[s, t] = {"helper": c, "hop": free[per * j:per * j + per], "codes": topo.engines(c, cores[t]),
                           "scales": topo.engines(c, cores[t])}
         n = len(far)
         if len(direct[s]) == 1:
-            road[s, direct[s][0]] = {"helper": None, "codes": far, "scales": far}
+            road[s, direct[s][0]] = {"helper": None, "codes": far, "scales": road[s, t0]["hop"]}
         else:
             h, q = n // 2, n // 4
             cs = [far[:h], far[h:h + q], far[h + q:]]
@@ -89,7 +87,8 @@ def make_plan(cores, topo):
             for i in range(3):
                 t = major[(major.index(s) + 1 + i) % len(major)]
                 road[s, t] = {"helper": None, "codes": cs[i], "scales": ss[i]}
-    return direct, major, slots, rising, place, road
+    return {"direct": direct, "major": major, "slots": slots, "rising": rising, "place": place, "road": road, "pos": pos,
+            "chunks": chunks, "lead": lead}
 
 
 def rank_program(g, core, T, topo):
@@ -99,10 +98,9 @@ def rank_program(g, core, T, topo):
     if rank is not None:
         sender(g, core, T, topo, cores, rank, plan)
         return
-    place, road = plan[4], plan[5]
-    for (s, t), r in road.items():
+    for (s, t), r in plan["road"].items():
         if r["helper"] == core:
-            helper(g, core, T, topo, cores, r, t, place[s])
+            helper(g, core, T, topo, cores, r, t, plan["place"][s])
 
 
 def helper(g, core, T, topo, cores, r, t, at):
@@ -119,7 +117,8 @@ def helper(g, core, T, topo, cores, r, t, at):
 
 
 def sender(g, core, T, topo, cores, s, plan):
-    direct, major, slots, rising, place, road = plan
+    direct, major, slots, rising = plan["direct"], plan["major"], plan["slots"], plan["rising"]
+    place, road, pos, chunks, lead = plan["place"], plan["road"], plan["pos"], plan["chunks"], plan["lead"]
     sem = T.sem
     V, S, X = g.vector, g.scalar, g.sync
     A = AluOpType
@@ -134,84 +133,63 @@ def sender(g, core, T, topo, cores, s, plan):
     def tock():
         V.wait_ge(sem.v, cnt["v"])
 
-    def col(t):
-        return CAP * t if up else CAP * (N - 1 - t)
-
+    for q in range(4):
+        (X, S)[q % 2].dma_start(T.raw[16 * q:16 * q + 16, :, :], T.send[:, :]).then_inc(sem.lsend, 16)
     X.dma_start(T.xs[:, :], T.x[:, :]).then_inc(sem.lx, 16)
     for q in range(4):
-        (S, X)[q % 2].dma_start(T.raw[16 * q:16 * q + 16, :, :], T.send[:, :]).then_inc(sem.lsend, 16)
-    for q in range(4):
-        X.dma_start(T.ml[16 * q:16 * q + 16, 0:16], T.mine[:, :]).then_inc(sem.llist, 16)
+        S.dma_start(T.ml[16 * q:16 * q + 16, 0:16], T.mine[:, :]).then_inc(sem.llist, 16)
         X.dma_start(T.ml[16 * q:16 * q + 16, 16:32], T.prev[:, :]).then_inc(sem.llist, 16)
 
-    g.iota(T.o3i[:, 0:3], [[256, 3]], CAP, 1).then_inc(sem.gi, 1)
-    g.iota(T.mki[:, 0:48], [[0, 3], [1, 16]], 128, -1).then_inc(sem.gi, 1)
-    g.iota(T.jv[:, 0:TC], [[1, TC]], 0, 0, allow_small_or_imprecise_dtypes=True).then_inc(sem.gi, 1)
+    g.iota(T.jv[:, 0:TC], [[1, TC]], 0, 0).then_inc(sem.gi, 1)
     tick(V.memset(T.inv[:, 0:768], FAR))
-    V.wait_ge(sem.gi, 3)
-    tick(V.tensor_copy(T.o3[:, 0:3], T.o3i[:, 0:3]))
-    tick(V.tensor_scalar(T.mkb[:, 0:48], T.mki[:, 0:48], 15, None, A.bitwise_and))
-    tock()
-    tick(V.tensor_scalar(T.mk[:, 0:48], T.mkb[:, 0:48], 0.0, None, A.is_equal))
 
     V.wait_ge(sem.lsend, 64)
-    src = T.raw[:, :, :] if up else T.raw[:, ::-1, :]
-    for p in (0, 64):
-        V.tensor_scalar(T.off[p:p + 64, 0:24], src, 4.0, 0.0, A.mult, A.max).then_inc(sem.offr, 1)
-
-    first = 4 * CAP if up else 0
-    last = first + 4 * CAP * N
-    for q in (V, S):
-        q.wait_ge(sem.lx, 16)
-        q.wait_ge(sem.offr, 2)
-    for t in range(4):
-        win = T.xs[:, t:4 * TC].indirect(T.off[:, 0:24])
-        if t < 2:
-            tick(V.tensor_copy(T.h[:, first + t:last:4], win))
-        else:
-            S.activation(T.h[:, first + t:last:4], win, copy).then_inc(sem.sg, 1)
-    V.wait_ge(sem.sg, 2)
-    tock()
-
-    relay = [t for t in range(N) if t != s and t not in direct[s]]
-
-    def double():
-        z, e = T.h[:, 0:4 * CAP], T.h[:, 4 * CAP * N:4 * W]
-        tick(V.tensor_copy(z, e) if up else V.tensor_copy(e, z))
-        tock()
-
-    def pack(a, b, which):
-        V.quantize_mx(T.qc[:, a:b], T.qs[:, a:b], T.h[:, 4 * a:4 * b]).then_inc(which, 1)
-
-    n2 = 0
-    if len(relay) == 2:
-        a = min(col(t) for t in relay)
-        b = max(col(t) for t in relay) + 128
-        pack(a, b, sem.q1)
-        double()
-        for lo, hi in ((0, a), (b, W)):
-            if hi > lo:
-                pack(lo, hi, sem.q2)
-                n2 += 1
+    if up:
+        parts = [(0, T.raw[:, s:N, :], N - s)] + ([(N - s, T.raw[:, 0:s, :], s)] if s else [])
     else:
-        double()
-        pack(0, W, sem.q1)
-    slot, at = place[s]
-    V.quantize_mx(T.lc[:, at:at + 128], T.ls[:, at:at + 128], T.h[:, 4 * col(s):4 * col(s) + 512]).then_inc(sem.ql, 1)
+        parts = [(0, T.raw[:, s - 1::-1, :], s), (s, T.raw[:, N - 1:s - 1:-1, :], N - s)]
+    for b0, src, nb in parts:
+        for p in (0, 64):
+            V.tensor_scalar(T.off[p:p + 64, 4 * b0:4 * b0 + 4 * nb], src, 4.0, 0.0, A.mult, A.max).then_inc(sem.offr, 1)
 
+    for q in (V, S):
+        q.wait_ge(sem.offr, 2 * len(parts))
+        q.wait_ge(sem.lx, 16)
+    for c, (b0, b1) in enumerate(chunks[s]):
+        for t in range(4):
+            win = T.xs[:, t:4 * TC].indirect(T.off[:, 4 * b0:4 * b1])
+            out = T.h[:, 4 * CAP * b0 + t:4 * CAP * b1:4]
+            if t < 2:
+                tick(V.tensor_copy(out, win))
+            else:
+                S.activation(out, win, copy).then_inc(sem["sg%d" % c], 1)
+        V.wait_ge(sem["sg%d" % c], 2)
+        tock()
+        a, b = CAP * b0, CAP * b1
+        V.quantize_mx(T.qc[:, a:b], T.qs[:, a:b], T.h[:, 4 * a:4 * b]).then_inc(sem["q%d" % (c + 1)], 1)
+    slot, at = place[s]
+    tick(V.tensor_copy(T.h[:, 4 * CAP * N:4 * CAP * (N + 1)], T.h[:, 0:4 * CAP]))
+    tock()
+    V.quantize_mx(T.lc[:, at:at + 128], T.ls[:, at:at + 128],
+                  T.h[:, 4 * CAP * (N - 1):4 * CAP * (N + 1)]).then_inc(sem.ql, 1)
+
+    t0 = lead[s]
+    others = [t for t in range(N) if t != s and t not in direct[s] and t != t0]
+    calls = [(False, [t0]), (False, others + direct[s])]
+    if s in major:
+        calls.append((True, [t0] + others + direct[s]))
+    else:
+        calls += [(True, [t0] + others), (True, direct[s])]
     local = 0
-    for step in range(4):
-        far, codes = step > 1, step in (1, 2)
-        if step == 0:
-            g.wait_ge(sem.q1, 1)
-        if step == 2 and n2:
-            g.wait_ge(sem.q2, n2)
+    for n, (codes, dests) in enumerate(calls):
+        if n < 2:
+            g.wait_ge(sem["q%d" % (n + 1)], 1)
         trs = []
-        for t in (direct[s] if far else relay):
-            r, c0 = road[s, t], col(t)
+        for t in dests:
+            r, c0 = road[s, t], CAP * pos[s, t]
+            far = r["helper"] is None
             es = r["hop"] if not far else r["codes"] if codes else r["scales"]
-            to = cores[t] if far else r["helper"]
-            rid, pid = topo.addr(to, core)
+            rid, pid = topo.addr(cores[t] if far else r["helper"], core)
             if codes:
                 a_ = T.qc[:, c0:c0 + 128].bitcast(dt.uint8)
                 b_ = (T.lc[:, at:at + 128] if far else T.hc[:, 0:128]).bitcast(dt.uint8)
@@ -230,15 +208,15 @@ def sender(g, core, T, topo, cores, s, plan):
         own.append(b + (CAP if r in rising else 0))
         pre.append(b + (0 if r in rising else CAP))
     V.wait_ge(sem.llist, 128)
-    for i in range(N):
-        for half, tab in ((0, own), (16, pre)):
-            o_, i_ = T.tm[:, 32 * i + half:32 * i + half + 16], T.ml[:, half:half + 16]
-            if i == 0:
-                tick(V.tensor_scalar(o_, i_, float(tab[0]), None, A.add))
-            else:
-                tick(V.tensor_scalar(o_, i_, float(CAP * i), float(tab[i] - tab[i - 1]), A.is_ge, A.mult))
+    steps = [[(i, tab[i] - tab[i - 1]) for i in range(1, N) if tab[i] != tab[i - 1]] for tab in (own, pre)]
+    for half, tab, st in ((0, own, steps[0]), (16, pre, steps[1])):
+        i_ = T.ml[:, half:half + 16]
+        tick(V.tensor_scalar(T.tm[:, 128 + half:144 + half], i_, float(tab[0]), None, A.add))
+        for j in range(4):
+            i, dl = st[j] if j < len(st) else (N, 0)
+            tick(V.tensor_scalar(T.tm[:, 32 * j + half:32 * j + half + 16], i_, float(CAP * i), float(dl), A.is_ge, A.mult))
     tock()
-    for lo, n in ((96, 96), (32, 32), (64, 32)):
+    for lo, n in ((64, 64), (32, 32), (128, 32)):
         tick(V.tensor_tensor(T.tm[:, 0:n], T.tm[:, 0:n], T.tm[:, lo:lo + n], A.add))
         tock()
     for p in (0, 64):
@@ -246,25 +224,21 @@ def sender(g, core, T, topo, cores, s, plan):
     V.wait_ge(sem.offo, 2)
     om, op = T.oo[:, 0:16], T.oo[:, 16:32]
 
-    tick(V.tensor_copy(T.inv[:, 0:768].indirect(om), T.jv[:, 0:TC]))
-    tock()
-    tick(V.tensor_copy(T.ge[:, 0:48], T.inv[:, 0:768].indirect(T.o3[:, 0:3])))
-    tock()
-    tick(V.tensor_tensor(T.gm[:, 0:48], T.ge[:, 0:48], T.mk[:, 0:48], A.mult))
-    tock()
+    V.wait_ge(sem.gi, 1)
+    V.tensor_copy(T.inv[:, 0:768].indirect(om), T.jv[:, 0:TC]).then_inc(sem.iv, 1)
+    X.wait_ge(sem.iv, 1)
     for k in range(3):
-        tick(V.tensor_reduce(T.rf[:, k:k + 1], T.gm[:, 16 * k:16 * k + 16], AxisListType.X, A.add))
-    tock()
-    V.tensor_copy(T.idx[:, 0:3], T.rf[:, 0:3]).then_inc(sem.idxr, 1)
+        w0 = 256 * k + CAP
+        X.dma_start(T.idx[:, k:k + 1], T.inv[0:1, w0:w0 + 128]).then_inc(sem.idxr, 16)
 
     wait_for = [sum(len(road[a, s]["codes"]) + len(road[a, s]["scales"]) for a in slots[k] if a != s) for k in range(3)]
     if s in major:
         early, order = [0, 1], [0, 1, 2]
-        pieces = {0: [(0, 512, "V"), (512, 768, "V")], 1: [(0, 512, "S"), (512, 768, "S")],
+        pieces = {0: [(0, 512, "V"), (512, 640, "V"), (640, 768, "S")], 1: [(0, 512, "S"), (512, 768, "S")],
                   2: [(0, 512, "V"), (512, 768, "S")]}
         soon = [(0, 0), (1, 0)]
         vq = [(0, 0), (0, 1), (0,), (2, 0), (1,), (2,)]
-        sq = [(1, 0), (0,), (1, 1), (1,), (2, 1), (2,)]
+        sq = [(1, 0), (0, 2), (0,), (1, 1), (1,), (2, 1), (2,)]
     else:
         early, order = [2], [2, 0, 1]
         pieces = {2: [(512, 768, "S"), (0, 256, "V"), (256, 512, "S")], 0: [(0, 512, "V"), (512, 768, "S")],
@@ -273,17 +247,22 @@ def sender(g, core, T, topo, cores, s, plan):
         vq = [(2, 1), (2,), (0, 0), (0,), (1, 0), (1,)]
         sq = [(2, 0), (2, 2), (2,), (0, 1), (0,), (1, 1), (1,)]
     todo = soon + [(k, i) for k in order for i in range(len(pieces[k])) if (k, i) not in soon]
-    bank = {}
+    bank, there = {}, []
+
+    def need(k):
+        if k not in there:
+            g.tensor.wait_ge(sem["arr%d" % k], wait_for[k])
+            there.append(k)
+
     g.tensor.wait_ge(sem.ql, 1)
     for k in early:
-        g.tensor.wait_ge(sem["arr%d" % k], wait_for[k])
+        need(k)
     for k, i in todo:
-        if len(bank) == len(soon):
-            for e in range(3):
-                if e not in early:
-                    g.tensor.wait_ge(sem["arr%d" % e], wait_for[e])
-        b = bank[k, i] = len(bank)
         a, z, who = pieces[k][i]
+        need(k)
+        for e in range(a // 256, (z + 255) // 256):
+            need(e)
+        b = bank[k, i] = len(bank)
         w0 = 256 * k + CAP
         g.tensor.matmul_mx(T["ps%d" % b][:, 0:z - a], T.lc[:, w0:w0 + 128], T.ls[:, w0:w0 + 128], T.lc[:, a:z], T.ls[:, a:z],
                            True, True).then_inc(sem["m%d" % b], 1)
@@ -315,7 +294,7 @@ def sender(g, core, T, topo, cores, s, plan):
     after(S, sq)
     V.wait_ge(sem.v, cnt["v"])
 
-    g.wait_ge(sem.idxr, 1)
+    g.wait_ge(sem.idxr, 48)
     for k in order:
         g.wait_ge(sem["yr%d" % k], 2)
         g.indirect_dma_start(out=T.y[:], out_offset=IndirectOffsetOnAxis(ap=T.idx[:, k:k + 1], axis=0),

from concourse.bass import DstId, RemoteDMATransfer, IndirectOffsetOnAxis
from concourse.mybir import dt, AluOpType, ActivationFunctionType

N, TC, CAP = 6, 256, 64
FAR = 512

SCRATCH = {
    "xs": ("sbuf", [128, 4 * TC], "bfloat16"),
    "raw": ("sbuf", [64, N, 4], "int32"),
    "off": ("sbuf", [128, 24], "uint16"),
    "h": ("sbuf", [128, 4 * CAP * (N + 1)], "bfloat16"),
    "qc": ("sbuf", [128, CAP * N], "float8_e4m3fn_x4"),
    "qs": ("sbuf", [128, CAP * N], "uint8"),
    "lc": ("sbuf", [128, 768], "float8_e4m3fn_x4"),
    "ls": ("sbuf", [128, 768], "uint8"),
    "hc": ("sbuf", [128, 128], "float8_e4m3fn_x4"),
    "hp": ("sbuf", [128, 128], "uint8"),
    "ml": ("sbuf", [64, 32], "int32"),
    "tm": ("sbuf", [64, 32 * 6], "int32"),
    "oo": ("sbuf", [128, 32], "uint16"),
    "jv": ("sbuf", [128, TC], "int32"),
    "inv": ("sbuf", [128, 768], "int32"),
    "idx": ("sbuf", [128, 4], "int32"),
}
for _k in range(3):
    SCRATCH["s%d" % _k] = ("sbuf", [128, 768], "float32")
    SCRATCH["yt%d" % _k] = ("sbuf", [128, 2 * TC], "float32")
for _k in range(7):
    SCRATCH["ps%d" % _k] = ("psum", [128, 512], "float32")

SEMAPHORES = ["lsend", "lx", "llist", "offr", "sg0", "sg1", "q1", "q2", "ql", "gi", "offo", "iv", "idxr", "v",
              "arr0", "arr1", "arr2", "loc", "st", "hcs", "hss", "hl",
              "sv0", "sv1", "sv2", "ss0", "ss1", "ss2", "yr0", "yr1", "yr2"] + ["m%d" % k for k in range(7)]


def bits(es):
    m = 0
    for e in es:
        m |= 1 << e
    return m


def make_plan(cores, topo):
    direct = [[t for t in range(N) if t != s and topo.may_write(cores[s], cores[t])] for s in range(N)]
    most = max(len(d) for d in direct)
    major = [s for s in range(N) if len(direct[s]) == most]
    minor = [s for s in range(N) if len(direct[s]) != most]
    slots = [(major[0], major[1]), (major[2], major[3]), (minor[0], minor[1])]
    rising = [a for a, b in slots]
    place, pos, chunks, lead = {}, {}, {}, {}
    for k in range(3):
        for j in range(2):
            place[slots[k][j]] = (k, 256 * k + 128 * j)
    road = {}
    for s in range(N):
        me = cores[s]
        relay = [t for t in range(N) if t != s and t not in direct[s]]
        for t in range(N):
            pos[s, t] = (t - 1 - s) % N if s in rising else (s - 1 - t) % N
        size, t0, front = min([(pos[s, t] + 2, t, True) for t in relay] + [(N - pos[s, t], t, False) for t in relay])
        lead[s] = t0
        chunks[s] = [(0, size), (size, N)] if front else [(N - size, N), (0, N - size)]
        flip = (major if s in major else minor).index(s) % 2
        sets = [[c for c in topo.cores_of(me) if c != me and topo.may_write(c, cores[relay[0]])
                 and (topo.die(c) != topo.die(me)) == bool(other)] for other in (0, 1)]
        half = (len(relay) + 1) // 2
        used = [0, 0]
        on = topo.engines(me, sets[0][0])
        far = topo.engines(me, cores[direct[s][0]])
        free = [e for e in on if e not in far] if len(relay) <= 2 else far + [e for e in on if e not in far]
        per = len(free) // len(relay)
        turn = [t0] + [t for t in relay if t != t0]
        for i, t in enumerate(relay):
            d = (0 if i < half else 1) ^ flip
            c = sets[d][used[d]]
            used[d] += 1
            j = turn.index(t)
            road[s, t] = {"helper": c, "hop": free[per * j:per * j + per], "codes": topo.engines(c, cores[t]),
                          "scales": topo.engines(c, cores[t])}
        n = len(far)
        if len(direct[s]) == 1:
            road[s, direct[s][0]] = {"helper": None, "codes": far, "scales": road[s, t0]["hop"]}
        else:
            h, q = n // 2, n // 4
            cs = [far[:h], far[h:h + q], far[h + q:]]
            ss = [far[h:], far[:q], far[q:h]]
            for i in range(3):
                t = major[(major.index(s) + 1 + i) % len(major)]
                road[s, t] = {"helper": None, "codes": cs[i], "scales": ss[i]}
    return {"direct": direct, "major": major, "slots": slots, "rising": rising, "place": place, "road": road, "pos": pos,
            "chunks": chunks, "lead": lead}


def rank_program(g, core, T, topo):
    cores = list(T.cores)
    plan = make_plan(cores, topo)
    rank = T.rank_of(core)
    if rank is not None:
        sender(g, core, T, topo, cores, rank, plan)
        return
    for (s, t), r in plan["road"].items():
        if r["helper"] == core:
            helper(g, core, T, topo, cores, r, t, plan["place"][s])


def helper(g, core, T, topo, cores, r, t, at):
    slot, base = at
    rid, pid = topo.addr(cores[t], core)
    arr = T.sem["arr%d" % slot]
    n = len(r["hop"])
    g.wait_ge(T.sem.hss, n)
    g.remote_dma(T.ls[:, base:base + 128], T.hp[:, 0:128], arr, T.sem.hl, pid, rid, bits(r["scales"]))
    g.wait_ge(T.sem.hcs, n)
    g.remote_dma(T.lc[:, base:base + 128].bitcast(dt.uint8), T.hc[:, 0:128].bitcast(dt.uint8), arr, T.sem.hl, pid, rid,
                 bits(r["codes"]))
    g.wait_ge(T.sem.hl, len(r["scales"]) + len(r["codes"]))


def sender(g, core, T, topo, cores, s, plan):
    direct, major, slots, rising = plan["direct"], plan["major"], plan["slots"], plan["rising"]
    place, road, pos, chunks, lead = plan["place"], plan["road"], plan["pos"], plan["chunks"], plan["lead"]
    sem = T.sem
    V, S, X = g.vector, g.scalar, g.sync
    A = AluOpType
    copy = ActivationFunctionType.Copy
    up = s in rising
    cnt = {"v": 0}

    def tick(ins):
        ins.then_inc(sem.v, 1)
        cnt["v"] += 1

    def tock():
        V.wait_ge(sem.v, cnt["v"])

    for q in range(4):
        (X, S)[q % 2].dma_start(T.raw[16 * q:16 * q + 16, :, :], T.send[:, :]).then_inc(sem.lsend, 16)
    X.dma_start(T.xs[:, :], T.x[:, :]).then_inc(sem.lx, 16)
    for q in range(4):
        S.dma_start(T.ml[16 * q:16 * q + 16, 0:16], T.mine[:, :]).then_inc(sem.llist, 16)
        X.dma_start(T.ml[16 * q:16 * q + 16, 16:32], T.prev[:, :]).then_inc(sem.llist, 16)

    g.iota(T.jv[:, 0:TC], [[1, TC]], 0, 0).then_inc(sem.gi, 1)
    tick(V.memset(T.inv[:, 0:768], FAR))

    V.wait_ge(sem.lsend, 64)
    if up:
        parts = [(0, T.raw[:, s:N, :], N - s)] + ([(N - s, T.raw[:, 0:s, :], s)] if s else [])
    else:
        parts = [(0, T.raw[:, s - 1::-1, :], s), (s, T.raw[:, N - 1:s - 1:-1, :], N - s)]
    for b0, src, nb in parts:
        for p in (0, 64):
            V.tensor_scalar(T.off[p:p + 64, 4 * b0:4 * b0 + 4 * nb], src, 4.0, 0.0, A.mult, A.max).then_inc(sem.offr, 1)

    for q in (V, S):
        q.wait_ge(sem.offr, 2 * len(parts))
        q.wait_ge(sem.lx, 16)
    for c, (b0, b1) in enumerate(chunks[s]):
        for t in range(4):
            win = T.xs[:, t:4 * TC].indirect(T.off[:, 4 * b0:4 * b1])
            out = T.h[:, 4 * CAP * b0 + t:4 * CAP * b1:4]
            if t < 2:
                tick(V.tensor_copy(out, win))
            else:
                S.activation(out, win, copy).then_inc(sem["sg%d" % c], 1)
        V.wait_ge(sem["sg%d" % c], 2)
        tock()
        a, b = CAP * b0, CAP * b1
        V.quantize_mx(T.qc[:, a:b], T.qs[:, a:b], T.h[:, 4 * a:4 * b]).then_inc(sem["q%d" % (c + 1)], 1)
    slot, at = place[s]
    tick(V.tensor_copy(T.h[:, 4 * CAP * N:4 * CAP * (N + 1)], T.h[:, 0:4 * CAP]))
    tock()
    V.quantize_mx(T.lc[:, at:at + 128], T.ls[:, at:at + 128],
                  T.h[:, 4 * CAP * (N - 1):4 * CAP * (N + 1)]).then_inc(sem.ql, 1)

    t0 = lead[s]
    others = [t for t in range(N) if t != s and t not in direct[s] and t != t0]
    calls = [(False, [t0]), (False, others + direct[s])]
    if s in major:
        calls.append((True, [t0] + others + direct[s]))
    else:
        calls += [(True, [t0] + others), (True, direct[s])]
    local = 0
    for n, (codes, dests) in enumerate(calls):
        if n < 2:
            g.wait_ge(sem["q%d" % (n + 1)], 1)
        trs = []
        for t in dests:
            r, c0 = road[s, t], CAP * pos[s, t]
            far = r["helper"] is None
            es = r["hop"] if not far else r["codes"] if codes else r["scales"]
            rid, pid = topo.addr(cores[t] if far else r["helper"], core)
            if codes:
                a_ = T.qc[:, c0:c0 + 128].bitcast(dt.uint8)
                b_ = (T.lc[:, at:at + 128] if far else T.hc[:, 0:128]).bitcast(dt.uint8)
            else:
                a_ = T.qs[:, c0:c0 + 128]
                b_ = T.ls[:, at:at + 128] if far else T.hp[:, 0:128]
            m_ = sem["arr%d" % slot] if far else sem.hcs if codes else sem.hss
            trs.append(RemoteDMATransfer(dst_ids=[DstId(rid=rid, pnc=pid)], dma_engine_mask=bits(es), remote_sem=m_,
                                         src=a_, dst=b_))
            local += len(es)
        g.remote_dma_fused(trs, local_sem=sem.loc)

    own, pre = [], []
    for r in range(N):
        b = place[r][1] - CAP * r
        own.append(b + (CAP if r in rising else 0))
        pre.append(b + (0 if r in rising else CAP))
    V.wait_ge(sem.llist, 128)
    steps = [[(i, tab[i] - tab[i - 1]) for i in range(1, N) if tab[i] != tab[i - 1]] for tab in (own, pre)]
    for half, tab, st in ((0, own, steps[0]), (16, pre, steps[1])):
        i_ = T.ml[:, half:half + 16]
        tick(V.tensor_scalar(T.tm[:, 128 + half:144 + half], i_, float(tab[0]), None, A.add))
        for j in range(4):
            i, dl = st[j] if j < len(st) else (N, 0)
            tick(V.tensor_scalar(T.tm[:, 32 * j + half:32 * j + half + 16], i_, float(CAP * i), float(dl), A.is_ge, A.mult))
    tock()
    for lo, n in ((64, 64), (32, 32), (128, 32)):
        tick(V.tensor_tensor(T.tm[:, 0:n], T.tm[:, 0:n], T.tm[:, lo:lo + n], A.add))
        tock()
    for p in (0, 64):
        V.tensor_copy(T.oo[p:p + 64, 0:32], T.tm[:, 0:32]).then_inc(sem.offo, 1)
    V.wait_ge(sem.offo, 2)
    om, op = T.oo[:, 0:16], T.oo[:, 16:32]

    V.wait_ge(sem.gi, 1)
    V.tensor_copy(T.inv[:, 0:768].indirect(om), T.jv[:, 0:TC]).then_inc(sem.iv, 1)
    X.wait_ge(sem.iv, 1)
    for k in range(3):
        w0 = 256 * k + CAP
        X.dma_start(T.idx[:, k:k + 1], T.inv[0:1, w0:w0 + 128]).then_inc(sem.idxr, 16)

    wait_for = [sum(len(road[a, s]["codes"]) + len(road[a, s]["scales"]) for a in slots[k] if a != s) for k in range(3)]
    if s in major:
        early, order = [0, 1], [0, 1, 2]
        pieces = {0: [(0, 512, "V"), (512, 640, "V"), (640, 768, "S")], 1: [(0, 512, "S"), (512, 768, "S")],
                  2: [(0, 512, "V"), (512, 768, "S")]}
        soon = [(0, 0), (1, 0)]
        vq = [(0, 0), (0, 1), (0,), (2, 0), (1,), (2,)]
        sq = [(1, 0), (0, 2), (0,), (1, 1), (1,), (2, 1), (2,)]
    else:
        early, order = [2], [2, 0, 1]
        pieces = {2: [(512, 768, "S"), (0, 256, "V"), (256, 512, "S")], 0: [(0, 512, "V"), (512, 768, "S")],
                  1: [(0, 512, "V"), (512, 768, "S")]}
        soon = [(2, 0)]
        vq = [(2, 1), (2,), (0, 0), (0,), (1, 0), (1,)]
        sq = [(2, 0), (2, 2), (2,), (0, 1), (0,), (1, 1), (1,)]
    todo = soon + [(k, i) for k in order for i in range(len(pieces[k])) if (k, i) not in soon]
    bank, there = {}, []

    def need(k):
        if k not in there:
            g.tensor.wait_ge(sem["arr%d" % k], wait_for[k])
            there.append(k)

    g.tensor.wait_ge(sem.ql, 1)
    for k in early:
        need(k)
    for k, i in todo:
        a, z, who = pieces[k][i]
        need(k)
        for e in range(a // 256, (z + 255) // 256):
            need(e)
        b = bank[k, i] = len(bank)
        w0 = 256 * k + CAP
        g.tensor.matmul_mx(T["ps%d" % b][:, 0:z - a], T.lc[:, w0:w0 + 128], T.ls[:, w0:w0 + 128], T.lc[:, a:z], T.ls[:, a:z],
                           True, True).then_inc(sem["m%d" % b], 1)

    def after(q, steps):
        for st in steps:
            k = st[0]
            sk, yk = T["s%d" % k], T["yt%d" % k]
            if len(st) == 2:
                a, z, w = pieces[k][st[1]]
                b = bank[k, st[1]]
                q.wait_ge(sem["m%d" % b], 1)
                if q is V:
                    q.tensor_copy(sk[:, a:z], T["ps%d" % b][:, 0:z - a]).then_inc(sem["sv%d" % k], 1)
                else:
                    q.activation(sk[:, a:z], T["ps%d" % b][:, 0:z - a], copy).then_inc(sem["ss%d" % k], 1)
                continue
            for w, name in (("V", "sv%d"), ("S", "ss%d")):
                n = len([p for p in pieces[k] if p[2] == w])
                if n:
                    q.wait_ge(sem[name % k], n)
            if q is V:
                q.tensor_copy(yk[:, 0:TC], sk[:, 0:768].indirect(om)).then_inc(sem["yr%d" % k], 1)
            else:
                q.activation(yk[:, TC:2 * TC], sk[:, 0:768].indirect(op), copy).then_inc(sem["yr%d" % k], 1)

    S.wait_ge(sem.offo, 2)
    after(V, vq)
    after(S, sq)
    V.wait_ge(sem.v, cnt["v"])

    g.wait_ge(sem.idxr, 48)
    for k in order:
        g.wait_ge(sem["yr%d" % k], 2)
        g.indirect_dma_start(out=T.y[:], out_offset=IndirectOffsetOnAxis(ap=T.idx[:, k:k + 1], axis=0),
                             in_=T["yt%d" % k][:, 0:2 * TC], in_offset=None, bounds_check=TC - 1,
                             oob_is_err=False).then_inc(sem.st, 16)
    g.wait_ge(sem.st, 48)
    g.wait_ge(sem.loc, local)
